import numpy as np
import ml_dtypes


def mxq(x, axis, fmt="e4m3"):
    dtype, down = {"e4m3": (ml_dtypes.float8_e4m3fn, 7), "e5m2": (ml_dtypes.float8_e5m2, 14)}[fmt]
    v = np.moveaxis(np.asarray(x, np.float32).astype(ml_dtypes.bfloat16).astype(np.float64), axis, -1)
    blocks = v.reshape(v.shape[:-1] + (-1, 32))
    amax = np.abs(blocks).max(-1, keepdims=True)
    byte = np.maximum(np.where(amax > 0, np.frexp(amax)[1] - 1 + 127, 0) - down, 1)
    scale = np.exp2(byte - 127.0)
    codes = (blocks / scale).astype(np.float32).astype(dtype).astype(np.float64)
    return np.moveaxis((codes * scale).reshape(v.shape), -1, axis)


WIDE = False


def mx_kscale(k):
    if not WIDE:
        return np.ones(k)
    levels = np.array([10, -10, 5, -5, 0])
    if k % 512:
        return np.exp2(np.random.permutation(np.resize(levels, k // 32))).repeat(32)
    a = np.empty((k // 512, 16))
    for p in range(k // 512):
        a[p, :8] = np.random.permutation(np.resize(levels, 8))
        for g in range(8):
            far = levels[np.abs(levels - a[p, g]) >= 10]
            a[p, g + 8] = far[np.random.randint(len(far))]
    return np.exp2(a.ravel()).repeat(32)


def f64(x):
    return np.asarray(x).astype(np.float64)


def striped(idx):
    return np.tile(idx.reshape(-1, 16).T, (8, 1)).astype(np.uint16)


def unstriped(offs):
    return offs[:16].T.reshape(-1).astype(np.int64)


E2M1 = np.array([0.0, 0.5, 1.0, 1.5, 2.0, 3.0, 4.0, 6.0, -0.0, -0.5, -1.0, -1.5, -2.0, -3.0, -4.0, -6.0])


def pack_weight(w, fmt):
    k, n = w.shape
    w = f64(np.asarray(w, np.float32).astype(ml_dtypes.bfloat16)).reshape(k // 32, 32, n)
    amax = np.abs(w).max(1)
    if fmt == "e4m3":
        byte = np.frexp(amax)[1] - 1 + 127 - 7
    else:
        mant, ex = np.frexp(amax / 6.0)
        byte = np.where(mant > 0.5, ex, ex - 1) + 127
    byte = np.clip(np.where(amax > 0, byte, 1), 1, 254)
    scaled = (w * np.exp2(127.0 - byte)[:, None, :]).reshape(k, n).astype(np.float32)
    by_word = np.ascontiguousarray(scaled.reshape(k // 512, 128, 4, n).transpose(0, 1, 3, 2))
    if fmt == "e4m3":
        words = by_word.astype(ml_dtypes.float8_e4m3fn).view(np.uint8)
    else:
        c = by_word.astype(ml_dtypes.float4_e2m1fn).view(np.uint8) & 0xF
        words = (c[..., 0::2] | (c[..., 1::2] << 4)).reshape(k // 512, 128, 2 * n)
    return np.ascontiguousarray(words), np.ascontiguousarray(byte.astype(np.uint8).reshape(k // 512, 16, n))


def unpack_weight(words, scales, fmt):
    g, _, n = scales.shape
    words = np.ascontiguousarray(words).reshape(g, 128, n, -1)
    if fmt == "e4m3":
        vals = words.view(ml_dtypes.float8_e4m3fn).astype(np.float64)
    else:
        nib = np.empty((g, 128, n, 4), np.uint8)
        nib[..., 0::2] = words & 0xF
        nib[..., 1::2] = words >> 4
        vals = E2M1[nib]
    vals = vals * np.repeat(np.exp2(scales.astype(np.float64) - 127.0), 8, axis=1)[..., None]
    return vals.transpose(0, 1, 3, 2).reshape(g * 512, n)


def gelu(v):
    return 0.5 * v * (1.0 + np.tanh(np.sqrt(2.0 / np.pi) * (v + 0.044715 * v**3)))


def striped8(idx):
    return np.concatenate([v.reshape(-1, 16).T for v in idx]).astype(np.uint16)


def unstriped8(offs):
    return np.stack([offs[16 * g:16 * g + 16].T.reshape(-1) for g in range(8)]).astype(np.int64)


def heads(h, wgt, idx8):
    r = np.arange(h.shape[0])
    return wgt[r // 4 % 128] * h[r[:, None], idx8[r % 512 // 64]]


def put_heads(h, wgs, idx8, t2):
    r = np.arange(h.shape[0])
    page = np.zeros((h.shape[0], t2))
    page[r[:, None], idx8[r % 512 // 64]] = wgs[r // 4 % 128] * h
    return page


K, T, S, H, T2, P, N = 1536, 2048, 1024, 512, 2048, 1024, 640


def setup_inputs():
    n = np.random.standard_normal
    s = mx_kscale(K)[:, None]
    u = mx_kscale(H)[:, None]
    d = {}
    d["tab_words"], d["tab_scales"] = pack_weight(n((K, T)) * s, "e4m3")
    d["offs"] = striped(np.random.permutation(T)[:S])
    d["w1"] = (1.6 * n((K, H)) / K**0.5 / s).astype(np.float32)
    d["gain"] = (np.exp(0.3 * n(H)) * u[:, 0]).astype(np.float32)
    d["wgs"] = np.repeat(np.random.uniform(0.5, 2.0, (8, S)), 16, axis=0).astype(np.float32)
    d["offs2"] = striped8(np.stack([np.random.permutation(T2)[:S] for _ in range(8)]))
    d["wgt"] = np.repeat(np.random.uniform(0.5, 2.0, (8, P)), 16, axis=0).astype(np.float32)
    d["offs3"] = striped8(np.stack([np.random.permutation(T2)[:P] for _ in range(8)]))
    d["press"] = (n((H, P)) * u).astype(np.float32)
    d["w2"] = (n((H, N)) / H**0.5 / u).astype(np.float32)
    d["w4_words"], d["w4_scales"] = pack_weight(n((H, N)) / H**0.5 / u, "e2m1")
    return d


def reference(tab_words, tab_scales, offs, w1, gain, wgs, offs2, wgt, offs3, press, w2, w4_words, w4_scales):
    v = unpack_weight(tab_words, tab_scales, "e4m3")[:, unstriped(offs)]
    y = mxq(f64(w1), 0, "e4m3").T @ v
    h = y / (1.0 + np.exp(-y)) * f64(gain)[:, None]
    page = put_heads(h, f64(wgs), unstriped8(offs2), T2)
    x = heads(page, f64(wgt), unstriped8(offs3))
    z = mxq(x - f64(press), 0, "e4m3")
    resp = mxq(f64(w2), 0, "e4m3").T @ z
    strain = unpack_weight(w4_words, w4_scales, "e2m1").T @ z
    return resp / (1.0 + np.abs(strain))

@@ -1,0 +1,277 @@
+from contextlib import ExitStack
+
+import concourse.mybir as mybir
+
+K, T, S, H, T2, M, N = 1536, 2048, 1024, 512, 2048, 1024, 640
+FLOPS = 2 * K * H * S + 2 * 2 * H * N * M
+
+F32 = mybir.dt.float32
+BF16 = mybir.dt.bfloat16
+I32 = mybir.dt.int32
+U32 = mybir.dt.uint32
+U16 = mybir.dt.uint16
+U8 = mybir.dt.uint8
+E4M3 = mybir.dt.float8_e4m3fn_x4
+E2M1 = mybir.dt.float4_e2m1fn_x4
+ACT = mybir.ActivationFunctionType
+ALU = mybir.AluOpType
+
+P = 128
+PACK = 4
+PASSES = K // (P * PACK)
+HALF = 512
+CHUNKS = [(0, 128), (128, 128), (256, 256), (512, 256), (768, 256)]
+N_TILES = N // P
+
+
+def tile_list_chamber_session_response_kernel(
+    tc, tab_words, tab_scales, offs, w1, gain, wgs, offs2, wgt, offs3, press, w2, w4_words, w4_scales, out
+):
+    nc = tc.nc
+    with ExitStack() as ctx:
+        keep = ctx.enter_context(tc.tile_pool(name="keep", bufs=1))
+        ring2 = ctx.enter_context(tc.tile_pool(name="ring2", bufs=2))
+        ring3 = ctx.enter_context(tc.tile_pool(name="ring3", bufs=3))
+        ring4 = ctx.enter_context(tc.tile_pool(name="ring4", bufs=4))
+        banks5 = ctx.enter_context(tc.psum_pool(name="banks5", bufs=5))
+        banks3 = ctx.enter_context(tc.psum_pool(name="banks3", bufs=3))
+
+        pick = keep.tile([P, S // 16], U16, name="pick")
+        seat = keep.tile([P, S // 16], U16, name="seat")
+        session = keep.tile([P, M // 16], U16, name="session")
+
+        def entries(lists, first, count):
+            return lists[:, first // 16 : (first + count) // 16]
+
+        tab_planes = keep.tile([P, T], U8, name="tab_planes", align_bytes=64)
+        w4_plane = keep.tile([P, N], U8, name="w4_plane", align_bytes=64)
+        nc.vector.memset(tab_planes[:].bitcast(I32), 0)
+        nc.vector.memset(w4_plane[:].bitcast(I32), 0)
+        pages = [keep.tile([P, T2], F32, name="page%d" % t) for t in range(PACK)]
+        for page in pages:
+            nc.vector.memset(page[:].bitcast(I32), 0)
+
+        warm = keep.tile([P, 2], F32, name="warm")
+        nc.vector.memset(warm[:], 0.0)
+        nc.scalar.activation(out=warm[:, 1:2], in_=warm[:, 0:1], func=ACT.Silu)
+
+        tabs = [keep.tile([P, T], U32, name="tab%d" % a, align_bytes=64) for a in range(PASSES)]
+        w1_raw = [ring3.tile([P, PACK, H], F32, name="w1_raw%d" % a, tag="wide") for a in range(PASSES)]
+        gain_sb = keep.tile([P, PACK], F32, name="gain_sb")
+        wgs_sb = [keep.tile([P, HALF], F32, name="wgs_sb%d" % b) for b in range(2)]
+        wgt_sb = keep.tile([P, M], F32, name="wgt_sb")
+        press_sb = keep.tile([P, PACK, M], F32, name="press_sb")
+        w2_raw = keep.tile([P, PACK, N], F32, name="w2_raw")
+        w4_codes = keep.tile([P, 2 * N], U8, name="w4_codes", align_bytes=64)
+
+        def load_tab(a):
+            nc.sync.dma_start(out=tabs[a][:].bitcast(I32), in_=tab_words[a].rearrange("p n t -> p (n t)").bitcast(I32))
+
+        def load_w1(a):
+            rows = w1[a * P * PACK : (a + 1) * P * PACK, :]
+            nc.sync.dma_start(out=w1_raw[a][:], in_=rows.rearrange("(p j) c -> p j c", j=PACK))
+
+        load_tab(0)
+        for quad in range(4):
+            nc.sync.dma_start(
+                out=tab_planes[32 * quad : 32 * quad + 4 * PASSES, :].bitcast(I32),
+                in_=tab_scales[:, 4 * quad : 4 * quad + 4, :].bitcast(I32),
+            )
+        nc.sync.dma_start(pick[:], offs)
+        load_w1(0)
+        load_tab(1)
+        load_w1(1)
+        nc.sync.dma_start(out=gain_sb[:], in_=gain.rearrange("(p t) -> p t", t=PACK))
+        load_w1(2)
+        nc.sync.dma_start(seat[:], offs2)
+        load_tab(2)
+        for b in range(2):
+            nc.sync.dma_start(out=wgs_sb[b][:], in_=wgs[:, b * HALF : (b + 1) * HALF])
+        nc.sync.dma_start(out=w2_raw[:], in_=w2.rearrange("(p j) n -> p j n", j=PACK))
+        nc.sync.dma_start(session[:], offs3)
+        nc.sync.dma_start(out=wgt_sb[:], in_=wgt)
+        nc.sync.dma_start(out=press_sb[:], in_=press.rearrange("(p t) m -> p t m", t=PACK))
+        nc.sync.dma_start(out=w4_codes[:].bitcast(I32), in_=w4_words[0].bitcast(I32))
+        for quad in range(4):
+            nc.sync.dma_start(
+                out=w4_plane[32 * quad : 32 * quad + 4, :].bitcast(I32),
+                in_=w4_scales[0, 4 * quad : 4 * quad + 4, :].bitcast(I32),
+            )
+
+        v_codes = [keep.tile([P, S], U32, name="v_codes%d" % a, align_bytes=64) for a in range(PASSES)]
+        v_planes = keep.tile([P, S], U8, name="v_planes", align_bytes=64)
+        w1_codes = [keep.tile([P, H], U32, name="w1_codes%d" % a, align_bytes=64) for a in range(PASSES)]
+        w1_plane = [keep.tile([P, H], U8, name="w1_plane%d" % a, align_bytes=64) for a in range(PASSES)]
+
+        def gather_words(a, first, count):
+            nc.vector.tensor_copy(v_codes[a][:, first : first + count], tabs[a][:].indirect(entries(pick, first, count)))
+
+        def quantise_w1(a):
+            source = w1_raw[a][:].rearrange("p j (m t) -> p m j t", t=PACK)
+            for u in range(2):
+                rounded = ring4.tile([P, 2, P, PACK], BF16, name="w1_rounded", align_bytes=64)
+                target = rounded[:].rearrange("p t m j -> p m j t")
+                if a == PASSES - 1 and u == 0:
+                    nc.vector.tensor_copy(out=target, in_=source[:, :, :, 2 * u : 2 * u + 2])
+                else:
+                    nc.scalar.copy(out=target, in_=source[:, :, :, 2 * u : 2 * u + 2])
+                cols = slice(2 * u * P, 2 * (u + 1) * P)
+                nc.vector.quantize_mx(
+                    out=w1_codes[a][:, cols].bitcast(E4M3),
+                    scales=w1_plane[a][:, cols],
+                    in_=rounded[:].rearrange("p t m j -> p (t m j)"),
+                )
+
+        gather_words(0, 0, S)
+        nc.vector.tensor_copy(v_planes[:], tab_planes[:].indirect(pick[:]))
+        quantise_w1(0)
+        gather_words(1, 0, S)
+        quantise_w1(1)
+        quantise_w1(2)
+        gather_words(2, 0, HALF)
+        gather_words(2, HALF, HALF)
+
+        units = [(b, t) for b in range(2) for t in range(PACK)]
+        y = {}
+        for i, unit in enumerate(units):
+            y[unit] = banks5.tile([P, HALF], F32, name="bank5") if i < 5 else banks3.tile([P, HALF], F32, name="bank3")
+        for a in range(PASSES):
+            for b, t in units:
+                cols = slice(b * HALF, (b + 1) * HALF)
+                rows = slice(t * P, (t + 1) * P)
+                nc.tensor.matmul_mx(
+                    out=y[b, t][:],
+                    lhsT=w1_codes[a][:, rows].bitcast(E4M3),
+                    lhsT_scale=w1_plane[a][:, rows],
+                    rhs=v_codes[a][:, cols].bitcast(E4M3),
+                    rhs_scale=v_planes[4 * a : P, cols],
+                    start=(a == 0),
+                    stop=(a == PASSES - 1),
+                )
+        for b, t in units:
+            factor = ring4.tile([P, HALF], F32, name="factor")
+            nc.scalar.activation(out=factor[:], in_=wgs_sb[b][:], func=ACT.Copy, scale=gain_sb[:, t : t + 1])
+            silu = ring4.tile([P, HALF], F32, name="silu")
+            nc.scalar.activation(out=silu[:], in_=y[b, t][:], func=ACT.Silu)
+            nc.vector.tensor_tensor(pages[t][:].indirect(entries(seat, b * HALF, HALF)), silu[:], factor[:], ALU.mult)
+
+        nc.scalar.activation(out=warm[:, 1:2], in_=silu[:, 0:1], func=ACT.Abs_reciprocal_sqrt, bias=1.0)
+
+        w2_rounded = keep.tile([P, N, PACK], BF16, name="w2_rounded", align_bytes=64)
+        w2_codes = keep.tile([P, N], U32, name="w2_codes", align_bytes=64)
+        w2_plane = keep.tile([P, N], U8, name="w2_plane", align_bytes=64)
+        nc.scalar.copy(
+            out=w2_rounded[:].rearrange("p (c i) j -> p c j i", i=4),
+            in_=w2_raw[:].rearrange("p j (c i) -> p c j i", i=4),
+        )
+        for first, last in ((0, 512), (512, N)):
+            nc.vector.quantize_mx(
+                out=w2_codes[:, first:last].bitcast(E4M3),
+                scales=w2_plane[:, first:last],
+                in_=w2_rounded[:, first:last, :].rearrange("p n j -> p (n j)"),
+            )
+
+        z_codes = keep.tile([P, M], U32, name="z_codes", align_bytes=64)
+        z_plane = keep.tile([P, M], U8, name="z_plane", align_bytes=64)
+        damp = [keep.tile([P, N_TILES, HALF], F32, name="damp%d" % b) for b in range(2)]
+        chunks = len(CHUNKS)
+        x = {}
+        z = {}
+
+        def read_page(c, t):
+            first, width = CHUNKS[c]
+            if t == 0:
+                x[c] = ring2.tile([P, PACK, width], F32, name="x")
+            nc.vector.tensor_tensor(
+                x[c][:, t, :],
+                pages[t][:].indirect(entries(session, first, width)),
+                wgt_sb[:, first : first + width],
+                ALU.mult,
+            )
+
+        def subtract(c):
+            first, width = CHUNKS[c]
+            z[c] = ring2.tile([P, width, PACK], BF16, name="z", align_bytes=64)
+            nc.vector.tensor_tensor(
+                z[c][:].rearrange("p (c i) t -> p c t i", i=4),
+                x[c][:].rearrange("p t (c i) -> p c t i", i=4),
+                press_sb[:, :, first : first + width].rearrange("p t (c i) -> p c t i", i=4),
+                ALU.subtract,
+            )
+
+        def quantise_z(c):
+            first, width = CHUNKS[c]
+            cols = slice(first, first + width)
+            nc.vector.quantize_mx(
+                out=z_codes[:, cols].bitcast(E4M3), scales=z_plane[:, cols], in_=z[c][:].rearrange("p m t -> p (m t)")
+            )
+
+        def groups(width):
+            step = HALF // width
+            return [(lo, min(lo + step, N_TILES)) for lo in range(0, N_TILES, step)]
+
+        def damping(c):
+            first, width = CHUNKS[c]
+            cols = slice(first, first + width)
+            inner = slice(first % HALF, first % HALF + width)
+            parts = []
+            for lo, hi in groups(width):
+                strain = banks3.tile([P, hi - lo, width], F32, name="bank3")
+                for n in range(lo, hi):
+                    nc.tensor.matmul_mx(
+                        out=strain[:, n - lo, :],
+                        lhsT=w4_codes[:, 2 * n * P : 2 * (n + 1) * P].bitcast(E2M1),
+                        lhsT_scale=w4_plane[:, n * P : (n + 1) * P],
+                        rhs=z_codes[:, cols].bitcast(E4M3),
+                        rhs_scale=z_plane[:, cols],
+                        start=True,
+                        stop=True,
+                    )
+                part = damp[first // HALF][:, lo:hi, inner]
+                nc.scalar.activation(out=part, in_=strain[:], func=ACT.Abs)
+                parts.append(part)
+            if c + 1 < chunks:
+                parts = [damp[first // HALF][:, :, inner]]
+            for part in parts:
+                nc.scalar.activation(out=part, in_=part, func=ACT.Abs_reciprocal_sqrt, bias=1.0)
+            for part in parts:
+                nc.scalar.activation(out=part, in_=part, func=ACT.Square)
+
+        def respond(lo, hi, first, width):
+            cols = slice(first, first + width)
+            resp = banks5.tile([P, hi - lo, width], F32, name="bank5")
+            for n in range(lo, hi):
+                nc.tensor.matmul_mx(
+                    out=resp[:, n - lo, :],
+                    lhsT=w2_codes[:, n * P : (n + 1) * P].bitcast(E4M3),
+                    lhsT_scale=w2_plane[:, n * P : (n + 1) * P],
+                    rhs=z_codes[:, cols].bitcast(E4M3),
+                    rhs_scale=z_plane[:, cols],
+                    start=True,
+                    stop=True,
+                )
+            result = ring4.tile([P, hi - lo, width], F32, name="result")
+            inner = slice(first % HALF, first % HALF + width)
+            nc.vector.tensor_tensor(result[:], resp[:], damp[first // HALF][:, lo:hi, inner], ALU.mult)
+            nc.sync.dma_start(out=out[lo * P : hi * P, cols].rearrange("(n p) m -> p n m", p=P), in_=result[:])
+
+        for t in range(PACK):
+            read_page(0, t)
+        for c in range(chunks):
+            more = c + 1 < chunks
+            if more:
+                read_page(c + 1, 0)
+            subtract(c)
+            if more:
+                read_page(c + 1, 1)
+            quantise_z(c)
+            damping(c)
+            if more:
+                read_page(c + 1, 2)
+                read_page(c + 1, 3)
+        for n in range(N_TILES):
+            respond(n, n + 1, 0, HALF)
+        for first, width in CHUNKS:
+            if first >= HALF:
+                for lo, hi in groups(width):
+                    respond(lo, hi, first, width)

@@ -45,14 +45,14 @@ def tile_list_chamber_session_response_kernel(
 
         tab_planes = keep.tile([P, T], U8, name="tab_planes", align_bytes=64)
         w4_plane = keep.tile([P, N], U8, name="w4_plane", align_bytes=64)
-        nc.vector.memset(tab_planes[:].bitcast(I32), 0)
-        nc.vector.memset(w4_plane[:].bitcast(I32), 0)
+        nc.gpsimd.memset(tab_planes[:].bitcast(I32), 0)
+        nc.gpsimd.memset(w4_plane[:].bitcast(I32), 0)
         pages = [keep.tile([P, T2], F32, name="page%d" % t) for t in range(PACK)]
         for page in pages:
             nc.vector.memset(page[:].bitcast(I32), 0)
 
         warm = keep.tile([P, 2], F32, name="warm")
-        nc.vector.memset(warm[:], 0.0)
+        nc.gpsimd.memset(warm[:], 0.0)
         nc.scalar.activation(out=warm[:, 1:2], in_=warm[:, 0:1], func=ACT.Silu)
 
         tabs = [keep.tile([P, T], U32, name="tab%d" % a, align_bytes=64) for a in range(PASSES)]
@@ -72,15 +72,15 @@ def tile_list_chamber_session_response_kernel(
             nc.sync.dma_start(out=w1_raw[a][:], in_=rows.rearrange("(p j) c -> p j c", j=PACK))
 
         load_tab(0)
+        nc.sync.dma_start(pick[:], offs)
+        load_w1(0)
         for quad in range(4):
             nc.sync.dma_start(
                 out=tab_planes[32 * quad : 32 * quad + 4 * PASSES, :].bitcast(I32),
                 in_=tab_scales[:, 4 * quad : 4 * quad + 4, :].bitcast(I32),
             )
-        nc.sync.dma_start(pick[:], offs)
-        load_w1(0)
-        load_tab(1)
         load_w1(1)
+        load_tab(1)
         nc.sync.dma_start(out=gain_sb[:], in_=gain.rearrange("(p t) -> p t", t=PACK))
         load_w1(2)
         nc.sync.dma_start(seat[:], offs2)
@@ -135,8 +135,8 @@ def tile_list_chamber_session_response_kernel(
         y = {}
         for i, unit in enumerate(units):
             y[unit] = banks5.tile([P, HALF], F32, name="bank5") if i < 5 else banks3.tile([P, HALF], F32, name="bank3")
-        for a in range(PASSES):
-            for b, t in units:
+        for b, a, t in [(b, a, t) for b in range(2) for a in range(PASSES) for t in range(PACK)]:
+            if True:
                 cols = slice(b * HALF, (b + 1) * HALF)
                 rows = slice(t * P, (t + 1) * P)
                 nc.tensor.matmul_mx(
@@ -149,7 +149,7 @@ def tile_list_chamber_session_response_kernel(
                     stop=(a == PASSES - 1),
                 )
         for b, t in units:
-            factor = ring4.tile([P, HALF], F32, name="factor")
+            factor = ring2.tile([P, HALF], F32, name="factor")
             nc.scalar.activation(out=factor[:], in_=wgs_sb[b][:], func=ACT.Copy, scale=gain_sb[:, t : t + 1])
             silu = ring4.tile([P, HALF], F32, name="silu")
             nc.scalar.activation(out=silu[:], in_=y[b, t][:], func=ACT.Silu)
@@ -161,8 +161,8 @@ def tile_list_chamber_session_response_kernel(
         w2_codes = keep.tile([P, N], U32, name="w2_codes", align_bytes=64)
         w2_plane = keep.tile([P, N], U8, name="w2_plane", align_bytes=64)
         nc.scalar.copy(
-            out=w2_rounded[:].rearrange("p (c i) j -> p c j i", i=4),
-            in_=w2_raw[:].rearrange("p j (c i) -> p c j i", i=4),
+            out=w2_rounded[:].rearrange("p (c i) j -> p c j i", i=2),
+            in_=w2_raw[:].rearrange("p j (c i) -> p c j i", i=2),
         )
         for first, last in ((0, 512), (512, N)):
             nc.vector.quantize_mx(
@@ -193,9 +193,9 @@ def tile_list_chamber_session_response_kernel(
             first, width = CHUNKS[c]
             z[c] = ring2.tile([P, width, PACK], BF16, name="z", align_bytes=64)
             nc.vector.tensor_tensor(
-                z[c][:].rearrange("p (c i) t -> p c t i", i=4),
-                x[c][:].rearrange("p t (c i) -> p c t i", i=4),
-                press_sb[:, :, first : first + width].rearrange("p t (c i) -> p c t i", i=4),
+                z[c][:].rearrange("p (c i) t -> p c t i", i=2),
+                x[c][:].rearrange("p t (c i) -> p c t i", i=2),
+                press_sb[:, :, first : first + width].rearrange("p t (c i) -> p c t i", i=2),
                 ALU.subtract,
             )
 
@@ -231,7 +231,7 @@ def tile_list_chamber_session_response_kernel(
                 nc.scalar.activation(out=part, in_=strain[:], func=ACT.Abs)
                 parts.append(part)
             if c + 1 < chunks:
-                parts = [damp[first // HALF][:, :, inner]]
+                parts = [damp[first // HALF][:, : N_TILES - 1, inner], damp[first // HALF][:, N_TILES - 1 :, inner]]
             for part in parts:
                 nc.scalar.activation(out=part, in_=part, func=ACT.Abs_reciprocal_sqrt, bias=1.0)
             for part in parts:
@@ -250,10 +250,9 @@ def tile_list_chamber_session_response_kernel(
                     start=True,
                     stop=True,
                 )
-            result = ring4.tile([P, hi - lo, width], F32, name="result")
-            inner = slice(first % HALF, first % HALF + width)
-            nc.vector.tensor_tensor(result[:], resp[:], damp[first // HALF][:, lo:hi, inner], ALU.mult)
-            nc.sync.dma_start(out=out[lo * P : hi * P, cols].rearrange("(n p) m -> p n m", p=P), in_=result[:])
+            part = damp[first // HALF][:, lo:hi, first % HALF : first % HALF + width]
+            nc.vector.tensor_tensor(part, resp[:], part, ALU.mult)
+            nc.sync.dma_start(out=out[lo * P : hi * P, cols].rearrange("(n p) m -> p n m", p=P), in_=part)
 
         for t in range(PACK):
             read_page(0, t)

@@ -19,9 +19,14 @@ ALU = mybir.AluOpType
 P = 128
 PACK = 4
 PASSES = K // (P * PACK)
-HALF = 512
-CHUNKS = [(0, 128), (128, 128), (256, 256), (512, 256), (768, 256)]
+QUADRANTS = 4
+GROUP = 16
+BANK = 512
+HALVES = S // BANK
+CHUNK = 256
+CHUNKS = M // CHUNK
 N_TILES = N // P
+TILE_GROUPS = [(lo, min(lo + BANK // CHUNK, N_TILES)) for lo in range(0, N_TILES, BANK // CHUNK)]
 
 
 def tile_list_chamber_session_response_kernel(
@@ -30,51 +35,52 @@ def tile_list_chamber_session_response_kernel(
     nc = tc.nc
     with ExitStack() as ctx:
         keep = ctx.enter_context(tc.tile_pool(name="keep", bufs=1))
-        ring2 = ctx.enter_context(tc.tile_pool(name="ring2", bufs=2))
-        ring3 = ctx.enter_context(tc.tile_pool(name="ring3", bufs=3))
-        ring4 = ctx.enter_context(tc.tile_pool(name="ring4", bufs=4))
-        banks5 = ctx.enter_context(tc.psum_pool(name="banks5", bufs=5))
-        banks3 = ctx.enter_context(tc.psum_pool(name="banks3", bufs=3))
+        pairs = ctx.enter_context(tc.tile_pool(name="pairs", bufs=2))
+        triples = ctx.enter_context(tc.tile_pool(name="triples", bufs=len(TILE_GROUPS)))
+        fours = ctx.enter_context(tc.tile_pool(name="fours", bufs=PACK))
+        resp_banks = ctx.enter_context(tc.psum_pool(name="resp_banks", bufs=4))
+        strain_banks = ctx.enter_context(tc.psum_pool(name="strain_banks", bufs=4))
 
-        pick = keep.tile([P, S // 16], U16, name="pick")
-        seat = keep.tile([P, S // 16], U16, name="seat")
-        session = keep.tile([P, M // 16], U16, name="session")
+        pick = keep.tile([P, S // GROUP], U16, name="pick")
+        seat = keep.tile([P, S // GROUP], U16, name="seat")
+        session = keep.tile([P, M // GROUP], U16, name="session")
 
         def entries(lists, first, count):
-            return lists[:, first // 16 : (first + count) // 16]
+            return lists[:, first // GROUP : (first + count) // GROUP]
 
         tab_planes = keep.tile([P, T], U8, name="tab_planes", align_bytes=64)
         w4_plane = keep.tile([P, N], U8, name="w4_plane", align_bytes=64)
         nc.gpsimd.memset(tab_planes[:].bitcast(I32), 0)
         nc.gpsimd.memset(w4_plane[:].bitcast(I32), 0)
         pages = [keep.tile([P, T2], F32, name="page%d" % t) for t in range(PACK)]
-        for page in pages:
+        for page in pages[: PACK // 2]:
             nc.vector.memset(page[:].bitcast(I32), 0)
-
         warm = keep.tile([P, 2], F32, name="warm")
         nc.gpsimd.memset(warm[:], 0.0)
         nc.scalar.activation(out=warm[:, 1:2], in_=warm[:, 0:1], func=ACT.Silu)
+        for page in pages[PACK // 2 :]:
+            nc.gpsimd.memset(page[:].bitcast(I32), 0)
 
         tabs = [keep.tile([P, T], U32, name="tab%d" % a, align_bytes=64) for a in range(PASSES)]
-        w1_raw = [ring3.tile([P, PACK, H], F32, name="w1_raw%d" % a, tag="wide") for a in range(PASSES)]
+        w1_raw = [keep.tile([P, PACK, H], F32, name="w1_raw%d" % a) for a in range(PASSES)]
         gain_sb = keep.tile([P, PACK], F32, name="gain_sb")
-        wgs_sb = [keep.tile([P, HALF], F32, name="wgs_sb%d" % b) for b in range(2)]
+        wgs_sb = [keep.tile([P, BANK], F32, name="wgs_sb%d" % b) for b in range(HALVES)]
         wgt_sb = keep.tile([P, M], F32, name="wgt_sb")
         press_sb = keep.tile([P, PACK, M], F32, name="press_sb")
         w2_raw = keep.tile([P, PACK, N], F32, name="w2_raw")
         w4_codes = keep.tile([P, 2 * N], U8, name="w4_codes", align_bytes=64)
 
         def load_tab(a):
-            nc.sync.dma_start(out=tabs[a][:].bitcast(I32), in_=tab_words[a].rearrange("p n t -> p (n t)").bitcast(I32))
+            nc.sync.dma_start(out=tabs[a][:].bitcast(I32), in_=tab_words[a].rearrange("p n i -> p (n i)").bitcast(I32))
 
         def load_w1(a):
             rows = w1[a * P * PACK : (a + 1) * P * PACK, :]
-            nc.sync.dma_start(out=w1_raw[a][:], in_=rows.rearrange("(p j) c -> p j c", j=PACK))
+            nc.sync.dma_start(out=w1_raw[a][:], in_=rows.rearrange("(p i) r -> p i r", i=PACK))
 
         load_tab(0)
         nc.sync.dma_start(pick[:], offs)
         load_w1(0)
-        for quad in range(4):
+        for quad in range(QUADRANTS):
             nc.sync.dma_start(
                 out=tab_planes[32 * quad : 32 * quad + 4 * PASSES, :].bitcast(I32),
                 in_=tab_scales[:, 4 * quad : 4 * quad + 4, :].bitcast(I32),
@@ -85,14 +91,14 @@ def tile_list_chamber_session_response_kernel(
         load_w1(2)
         nc.sync.dma_start(seat[:], offs2)
         load_tab(2)
-        for b in range(2):
-            nc.sync.dma_start(out=wgs_sb[b][:], in_=wgs[:, b * HALF : (b + 1) * HALF])
-        nc.sync.dma_start(out=w2_raw[:], in_=w2.rearrange("(p j) n -> p j n", j=PACK))
+        for b in range(HALVES):
+            nc.sync.dma_start(out=wgs_sb[b][:], in_=wgs[:, b * BANK : (b + 1) * BANK])
+        nc.sync.dma_start(out=w2_raw[:], in_=w2.rearrange("(p i) n -> p i n", i=PACK))
         nc.sync.dma_start(session[:], offs3)
         nc.sync.dma_start(out=wgt_sb[:], in_=wgt)
         nc.sync.dma_start(out=press_sb[:], in_=press.rearrange("(p t) m -> p t m", t=PACK))
         nc.sync.dma_start(out=w4_codes[:].bitcast(I32), in_=w4_words[0].bitcast(I32))
-        for quad in range(4):
+        for quad in range(QUADRANTS):
             nc.sync.dma_start(
                 out=w4_plane[32 * quad : 32 * quad + 4, :].bitcast(I32),
                 in_=w4_scales[0, 4 * quad : 4 * quad + 4, :].bitcast(I32),
@@ -107,10 +113,10 @@ def tile_list_chamber_session_response_kernel(
             nc.vector.tensor_copy(v_codes[a][:, first : first + count], tabs[a][:].indirect(entries(pick, first, count)))
 
         def quantise_w1(a):
-            source = w1_raw[a][:].rearrange("p j (m t) -> p m j t", t=PACK)
-            for u in range(2):
-                rounded = ring4.tile([P, 2, P, PACK], BF16, name="w1_rounded", align_bytes=64)
-                target = rounded[:].rearrange("p t m j -> p m j t")
+            source = w1_raw[a][:].rearrange("p i (c t) -> p c i t", t=PACK)
+            for u in range(PACK // 2):
+                w1_rounded = fours.tile([P, 2, P, PACK], BF16, name="w1_rounded", align_bytes=64)
+                target = w1_rounded[:].rearrange("p t c i -> p c i t")
                 if a == PASSES - 1 and u == 0:
                     nc.vector.tensor_copy(out=target, in_=source[:, :, :, 2 * u : 2 * u + 2])
                 else:
@@ -119,7 +125,7 @@ def tile_list_chamber_session_response_kernel(
                 nc.vector.quantize_mx(
                     out=w1_codes[a][:, cols].bitcast(E4M3),
                     scales=w1_plane[a][:, cols],
-                    in_=rounded[:].rearrange("p t m j -> p (t m j)"),
+                    in_=w1_rounded[:].rearrange("p t c i -> p (t c i)"),
                 )
 
         gather_words(0, 0, S)
@@ -128,95 +134,91 @@ def tile_list_chamber_session_response_kernel(
         gather_words(1, 0, S)
         quantise_w1(1)
         quantise_w1(2)
-        gather_words(2, 0, HALF)
-        gather_words(2, HALF, HALF)
+        for b in range(HALVES):
+            gather_words(2, b * BANK, BANK)
 
-        units = [(b, t) for b in range(2) for t in range(PACK)]
-        y = {}
-        for i, unit in enumerate(units):
-            y[unit] = banks5.tile([P, HALF], F32, name="bank5") if i < 5 else banks3.tile([P, HALF], F32, name="bank3")
-        for b, a, t in [(b, a, t) for b in range(2) for a in range(PASSES) for t in range(PACK)]:
-            if True:
-                cols = slice(b * HALF, (b + 1) * HALF)
-                rows = slice(t * P, (t + 1) * P)
-                nc.tensor.matmul_mx(
-                    out=y[b, t][:],
-                    lhsT=w1_codes[a][:, rows].bitcast(E4M3),
-                    lhsT_scale=w1_plane[a][:, rows],
-                    rhs=v_codes[a][:, cols].bitcast(E4M3),
-                    rhs_scale=v_planes[4 * a : P, cols],
-                    start=(a == 0),
-                    stop=(a == PASSES - 1),
+        y = [
+            [banks.tile([P, BANK], F32, name="bank") for t in range(PACK)] for banks in (resp_banks, strain_banks)
+        ]
+        for b in range(HALVES):
+            cols = slice(b * BANK, (b + 1) * BANK)
+            for a in range(PASSES):
+                for t in range(PACK):
+                    rows = slice(t * P, (t + 1) * P)
+                    nc.tensor.matmul_mx(
+                        out=y[b][t][:],
+                        lhsT=w1_codes[a][:, rows].bitcast(E4M3),
+                        lhsT_scale=w1_plane[a][:, rows],
+                        rhs=v_codes[a][:, cols].bitcast(E4M3),
+                        rhs_scale=v_planes[4 * a : P, cols],
+                        start=(a == 0),
+                        stop=(a == PASSES - 1),
+                    )
+        for b in range(HALVES):
+            for t in range(PACK):
+                factor = pairs.tile([P, BANK], F32, name="factor")
+                nc.scalar.activation(out=factor[:], in_=wgs_sb[b][:], func=ACT.Copy, scale=gain_sb[:, t : t + 1])
+                silu = fours.tile([P, BANK], F32, name="silu")
+                nc.scalar.activation(out=silu[:], in_=y[b][t][:], func=ACT.Silu)
+                nc.vector.tensor_tensor(
+                    pages[t][:].indirect(entries(seat, b * BANK, BANK)), silu[:], factor[:], ALU.mult
                 )
-        for b, t in units:
-            factor = ring2.tile([P, HALF], F32, name="factor")
-            nc.scalar.activation(out=factor[:], in_=wgs_sb[b][:], func=ACT.Copy, scale=gain_sb[:, t : t + 1])
-            silu = ring4.tile([P, HALF], F32, name="silu")
-            nc.scalar.activation(out=silu[:], in_=y[b, t][:], func=ACT.Silu)
-            nc.vector.tensor_tensor(pages[t][:].indirect(entries(seat, b * HALF, HALF)), silu[:], factor[:], ALU.mult)
-
         nc.scalar.activation(out=warm[:, 1:2], in_=silu[:, 0:1], func=ACT.Abs_reciprocal_sqrt, bias=1.0)
 
         w2_rounded = keep.tile([P, N, PACK], BF16, name="w2_rounded", align_bytes=64)
         w2_codes = keep.tile([P, N], U32, name="w2_codes", align_bytes=64)
         w2_plane = keep.tile([P, N], U8, name="w2_plane", align_bytes=64)
         nc.scalar.copy(
-            out=w2_rounded[:].rearrange("p (c i) j -> p c j i", i=2),
-            in_=w2_raw[:].rearrange("p j (c i) -> p c j i", i=2),
+            out=w2_rounded[:].rearrange("p (c e) i -> p c i e", e=2),
+            in_=w2_raw[:].rearrange("p i (c e) -> p c i e", e=2),
         )
-        for first, last in ((0, 512), (512, N)):
+        for first, last in ((0, BANK), (BANK, N)):
             nc.vector.quantize_mx(
                 out=w2_codes[:, first:last].bitcast(E4M3),
                 scales=w2_plane[:, first:last],
-                in_=w2_rounded[:, first:last, :].rearrange("p n j -> p (n j)"),
+                in_=w2_rounded[:, first:last, :].rearrange("p n i -> p (n i)"),
             )
 
         z_codes = keep.tile([P, M], U32, name="z_codes", align_bytes=64)
         z_plane = keep.tile([P, M], U8, name="z_plane", align_bytes=64)
-        damp = [keep.tile([P, N_TILES, HALF], F32, name="damp%d" % b) for b in range(2)]
-        chunks = len(CHUNKS)
+        result = [keep.tile([P, N_TILES, BANK], F32, name="result%d" % half) for half in range(M // BANK)]
         x = {}
         z = {}
 
+        def result_part(lo, hi, first, width):
+            return result[first // BANK][:, lo:hi, first % BANK : first % BANK + width]
+
         def read_page(c, t):
-            first, width = CHUNKS[c]
             if t == 0:
-                x[c] = ring2.tile([P, PACK, width], F32, name="x")
+                x[c] = pairs.tile([P, PACK, CHUNK], F32, name="x")
             nc.vector.tensor_tensor(
                 x[c][:, t, :],
-                pages[t][:].indirect(entries(session, first, width)),
-                wgt_sb[:, first : first + width],
+                pages[t][:].indirect(entries(session, c * CHUNK, CHUNK)),
+                wgt_sb[:, c * CHUNK : (c + 1) * CHUNK],
                 ALU.mult,
             )
 
         def subtract(c):
-            first, width = CHUNKS[c]
-            z[c] = ring2.tile([P, width, PACK], BF16, name="z", align_bytes=64)
+            z[c] = pairs.tile([P, CHUNK, PACK], BF16, name="z", align_bytes=64)
             nc.vector.tensor_tensor(
-                z[c][:].rearrange("p (c i) t -> p c t i", i=2),
-                x[c][:].rearrange("p t (c i) -> p c t i", i=2),
-                press_sb[:, :, first : first + width].rearrange("p t (c i) -> p c t i", i=2),
+                z[c][:].rearrange("p (c e) t -> p c t e", e=2),
+                x[c][:].rearrange("p t (c e) -> p c t e", e=2),
+                press_sb[:, :, c * CHUNK : (c + 1) * CHUNK].rearrange("p t (c e) -> p c t e", e=2),
                 ALU.subtract,
             )
 
         def quantise_z(c):
-            first, width = CHUNKS[c]
-            cols = slice(first, first + width)
+            cols = slice(c * CHUNK, (c + 1) * CHUNK)
             nc.vector.quantize_mx(
                 out=z_codes[:, cols].bitcast(E4M3), scales=z_plane[:, cols], in_=z[c][:].rearrange("p m t -> p (m t)")
             )
 
-        def groups(width):
-            step = HALF // width
-            return [(lo, min(lo + step, N_TILES)) for lo in range(0, N_TILES, step)]
+        root_chunk = CHUNKS - 2
 
         def damping(c):
-            first, width = CHUNKS[c]
-            cols = slice(first, first + width)
-            inner = slice(first % HALF, first % HALF + width)
-            parts = []
-            for lo, hi in groups(width):
-                strain = banks3.tile([P, hi - lo, width], F32, name="bank3")
+            cols = slice(c * CHUNK, (c + 1) * CHUNK)
+            for lo, hi in TILE_GROUPS:
+                strain = strain_banks.tile([P, hi - lo, CHUNK], F32, name="bank")
                 for n in range(lo, hi):
                     nc.tensor.matmul_mx(
                         out=strain[:, n - lo, :],
@@ -227,19 +229,18 @@ def tile_list_chamber_session_response_kernel(
                         start=True,
                         stop=True,
                     )
-                part = damp[first // HALF][:, lo:hi, inner]
-                nc.scalar.activation(out=part, in_=strain[:], func=ACT.Abs)
-                parts.append(part)
-            if c + 1 < chunks:
-                parts = [damp[first // HALF][:, : N_TILES - 1, inner], damp[first // HALF][:, N_TILES - 1 :, inner]]
+                nc.scalar.activation(out=result_part(lo, hi, c * CHUNK, CHUNK), in_=strain[:], func=ACT.Abs)
+            spans = TILE_GROUPS if c == CHUNKS - 1 else [(0, N_TILES - 1), (N_TILES - 1, N_TILES)]
+            parts = [result_part(lo, hi, c * CHUNK, CHUNK) for lo, hi in spans]
             for part in parts:
                 nc.scalar.activation(out=part, in_=part, func=ACT.Abs_reciprocal_sqrt, bias=1.0)
-            for part in parts:
-                nc.scalar.activation(out=part, in_=part, func=ACT.Square)
+            if c != root_chunk:
+                for part in parts:
+                    nc.scalar.activation(out=part, in_=part, func=ACT.Square)
 
-        def respond(lo, hi, first, width):
+        def response(lo, hi, first, width):
             cols = slice(first, first + width)
-            resp = banks5.tile([P, hi - lo, width], F32, name="bank5")
+            resp = resp_banks.tile([P, hi - lo, width], F32, name="bank")
             for n in range(lo, hi):
                 nc.tensor.matmul_mx(
                     out=resp[:, n - lo, :],
@@ -250,14 +251,18 @@ def tile_list_chamber_session_response_kernel(
                     start=True,
                     stop=True,
                 )
-            part = damp[first // HALF][:, lo:hi, first % HALF : first % HALF + width]
-            nc.vector.tensor_tensor(part, resp[:], part, ALU.mult)
-            nc.sync.dma_start(out=out[lo * P : hi * P, cols].rearrange("(n p) m -> p n m", p=P), in_=part)
+            return resp
+
+        def damp_and_store(values, lo, hi, first, width):
+            part = result_part(lo, hi, first, width)
+            nc.vector.tensor_tensor(part, values[:], part, ALU.mult)
+            rows = out[lo * P : hi * P, first : first + width]
+            nc.sync.dma_start(out=rows.rearrange("(n p) m -> p n m", p=P), in_=part)
 
         for t in range(PACK):
             read_page(0, t)
-        for c in range(chunks):
-            more = c + 1 < chunks
+        for c in range(CHUNKS):
+            more = c + 1 < CHUNKS
             if more:
                 read_page(c + 1, 0)
             subtract(c)
@@ -268,9 +273,18 @@ def tile_list_chamber_session_response_kernel(
             if more:
                 read_page(c + 1, 2)
                 read_page(c + 1, 3)
+
         for n in range(N_TILES):
-            respond(n, n + 1, 0, HALF)
-        for first, width in CHUNKS:
-            if first >= HALF:
-                for lo, hi in groups(width):
-                    respond(lo, hi, first, width)
+            damp_and_store(response(n, n + 1, 0, BANK), n, n + 1, 0, BANK)
+        first = root_chunk * CHUNK
+        halfway = []
+        for lo, hi in TILE_GROUPS:
+            resp = response(lo, hi, first, CHUNK)
+            once = triples.tile([P, hi - lo, CHUNK], F32, name="once")
+            nc.vector.tensor_tensor(once[:], resp[:], result_part(lo, hi, first, CHUNK), ALU.mult)
+            halfway.append(once)
+        for (lo, hi), once in zip(TILE_GROUPS, halfway):
+            damp_and_store(once, lo, hi, first, CHUNK)
+        first = (CHUNKS - 1) * CHUNK
+        for lo, hi in TILE_GROUPS:
+            damp_and_store(response(lo, hi, first, CHUNK), lo, hi, first, CHUNK)

from contextlib import ExitStack

import concourse.mybir as mybir

K, T, S, H, T2, M, N = 1536, 2048, 1024, 512, 2048, 1024, 640
FLOPS = 2 * K * H * S + 2 * 2 * H * N * M

F32 = mybir.dt.float32
BF16 = mybir.dt.bfloat16
I32 = mybir.dt.int32
U32 = mybir.dt.uint32
U16 = mybir.dt.uint16
U8 = mybir.dt.uint8
E4M3 = mybir.dt.float8_e4m3fn_x4
E2M1 = mybir.dt.float4_e2m1fn_x4
ACT = mybir.ActivationFunctionType
ALU = mybir.AluOpType

P = 128
PACK = 4
PASSES = K // (P * PACK)
QUADRANTS = 4
GROUP = 16
BANK = 512
HALVES = S // BANK
CHUNK = 256
CHUNKS = M // CHUNK
N_TILES = N // P
TILE_GROUPS = [(lo, min(lo + BANK // CHUNK, N_TILES)) for lo in range(0, N_TILES, BANK // CHUNK)]


def tile_list_chamber_session_response_kernel(
    tc, tab_words, tab_scales, offs, w1, gain, wgs, offs2, wgt, offs3, press, w2, w4_words, w4_scales, out
):
    nc = tc.nc
    with ExitStack() as ctx:
        keep = ctx.enter_context(tc.tile_pool(name="keep", bufs=1))
        pairs = ctx.enter_context(tc.tile_pool(name="pairs", bufs=2))
        triples = ctx.enter_context(tc.tile_pool(name="triples", bufs=len(TILE_GROUPS)))
        fours = ctx.enter_context(tc.tile_pool(name="fours", bufs=PACK))
        resp_banks = ctx.enter_context(tc.psum_pool(name="resp_banks", bufs=4))
        strain_banks = ctx.enter_context(tc.psum_pool(name="strain_banks", bufs=4))

        pick = keep.tile([P, S // GROUP], U16, name="pick")
        seat = keep.tile([P, S // GROUP], U16, name="seat")
        session = keep.tile([P, M // GROUP], U16, name="session")

        def entries(lists, first, count):
            return lists[:, first // GROUP : (first + count) // GROUP]

        tab_planes = keep.tile([P, T], U8, name="tab_planes", align_bytes=64)
        w4_plane = keep.tile([P, N], U8, name="w4_plane", align_bytes=64)
        nc.gpsimd.memset(tab_planes[:].bitcast(I32), 0)
        nc.gpsimd.memset(w4_plane[:].bitcast(I32), 0)
        pages = [keep.tile([P, T2], F32, name="page%d" % t) for t in range(PACK)]
        for page in pages[: PACK // 2]:
            nc.vector.memset(page[:].bitcast(I32), 0)
        warm = keep.tile([P, 2], F32, name="warm")
        nc.gpsimd.memset(warm[:], 0.0)
        nc.scalar.activation(out=warm[:, 1:2], in_=warm[:, 0:1], func=ACT.Silu)
        for page in pages[PACK // 2 :]:
            nc.gpsimd.memset(page[:].bitcast(I32), 0)

        tabs = [keep.tile([P, T], U32, name="tab%d" % a, align_bytes=64) for a in range(PASSES)]
        w1_raw = [keep.tile([P, PACK, H], F32, name="w1_raw%d" % a) for a in range(PASSES)]
        gain_sb = keep.tile([P, PACK], F32, name="gain_sb")
        wgs_sb = [keep.tile([P, BANK], F32, name="wgs_sb%d" % b) for b in range(HALVES)]
        wgt_sb = keep.tile([P, M], F32, name="wgt_sb")
        press_sb = keep.tile([P, PACK, M], F32, name="press_sb")
        w2_raw = keep.tile([P, PACK, N], F32, name="w2_raw")
        w4_codes = keep.tile([P, 2 * N], U8, name="w4_codes", align_bytes=64)

        def load_tab(a):
            nc.sync.dma_start(out=tabs[a][:].bitcast(I32), in_=tab_words[a].rearrange("p n i -> p (n i)").bitcast(I32))

        def load_w1(a):
            rows = w1[a * P * PACK : (a + 1) * P * PACK, :]
            nc.sync.dma_start(out=w1_raw[a][:], in_=rows.rearrange("(p i) r -> p i r", i=PACK))

        load_tab(0)
        nc.sync.dma_start(pick[:], offs)
        load_w1(0)
        for quad in range(QUADRANTS):
            nc.sync.dma_start(
                out=tab_planes[32 * quad : 32 * quad + 4 * PASSES, :].bitcast(I32),
                in_=tab_scales[:, 4 * quad : 4 * quad + 4, :].bitcast(I32),
            )
        load_w1(1)
        load_tab(1)
        nc.sync.dma_start(out=gain_sb[:], in_=gain.rearrange("(p t) -> p t", t=PACK))
        load_w1(2)
        nc.sync.dma_start(seat[:], offs2)
        load_tab(2)
        for b in range(HALVES):
            nc.sync.dma_start(out=wgs_sb[b][:], in_=wgs[:, b * BANK : (b + 1) * BANK])
        nc.sync.dma_start(out=w2_raw[:], in_=w2.rearrange("(p i) n -> p i n", i=PACK))
        nc.sync.dma_start(session[:], offs3)
        nc.sync.dma_start(out=wgt_sb[:], in_=wgt)
        nc.sync.dma_start(out=press_sb[:], in_=press.rearrange("(p t) m -> p t m", t=PACK))
        nc.sync.dma_start(out=w4_codes[:].bitcast(I32), in_=w4_words[0].bitcast(I32))
        for quad in range(QUADRANTS):
            nc.sync.dma_start(
                out=w4_plane[32 * quad : 32 * quad + 4, :].bitcast(I32),
                in_=w4_scales[0, 4 * quad : 4 * quad + 4, :].bitcast(I32),
            )

        v_codes = [keep.tile([P, S], U32, name="v_codes%d" % a, align_bytes=64) for a in range(PASSES)]
        v_planes = keep.tile([P, S], U8, name="v_planes", align_bytes=64)
        w1_codes = [keep.tile([P, H], U32, name="w1_codes%d" % a, align_bytes=64) for a in range(PASSES)]
        w1_plane = [keep.tile([P, H], U8, name="w1_plane%d" % a, align_bytes=64) for a in range(PASSES)]

        def gather_words(a, first, count):
            nc.vector.tensor_copy(v_codes[a][:, first : first + count], tabs[a][:].indirect(entries(pick, first, count)))

        def quantise_w1(a):
            source = w1_raw[a][:].rearrange("p i (c t) -> p c i t", t=PACK)
            for u in range(PACK // 2):
                w1_rounded = fours.tile([P, 2, P, PACK], BF16, name="w1_rounded", align_bytes=64)
                target = w1_rounded[:].rearrange("p t c i -> p c i t")
                if a == PASSES - 1 and u == 0:
                    nc.vector.tensor_copy(out=target, in_=source[:, :, :, 2 * u : 2 * u + 2])
                else:
                    nc.scalar.copy(out=target, in_=source[:, :, :, 2 * u : 2 * u + 2])
                cols = slice(2 * u * P, 2 * (u + 1) * P)
                nc.vector.quantize_mx(
                    out=w1_codes[a][:, cols].bitcast(E4M3),
                    scales=w1_plane[a][:, cols],
                    in_=w1_rounded[:].rearrange("p t c i -> p (t c i)"),
                )

        gather_words(0, 0, S)
        nc.vector.tensor_copy(v_planes[:], tab_planes[:].indirect(pick[:]))
        quantise_w1(0)
        gather_words(1, 0, S)
        quantise_w1(1)
        quantise_w1(2)
        for b in range(HALVES):
            gather_words(2, b * BANK, BANK)

        y = [
            [banks.tile([P, BANK], F32, name="bank") for t in range(PACK)] for banks in (resp_banks, strain_banks)
        ]
        for b in range(HALVES):
            cols = slice(b * BANK, (b + 1) * BANK)
            for a in range(PASSES):
                for t in range(PACK):
                    rows = slice(t * P, (t + 1) * P)
                    nc.tensor.matmul_mx(
                        out=y[b][t][:],
                        lhsT=w1_codes[a][:, rows].bitcast(E4M3),
                        lhsT_scale=w1_plane[a][:, rows],
                        rhs=v_codes[a][:, cols].bitcast(E4M3),
                        rhs_scale=v_planes[4 * a : P, cols],
                        start=(a == 0),
                        stop=(a == PASSES - 1),
                    )
        for b in range(HALVES):
            for t in range(PACK):
                factor = pairs.tile([P, BANK], F32, name="factor")
                nc.scalar.activation(out=factor[:], in_=wgs_sb[b][:], func=ACT.Copy, scale=gain_sb[:, t : t + 1])
                silu = fours.tile([P, BANK], F32, name="silu")
                nc.scalar.activation(out=silu[:], in_=y[b][t][:], func=ACT.Silu)
                nc.vector.tensor_tensor(
                    pages[t][:].indirect(entries(seat, b * BANK, BANK)), silu[:], factor[:], ALU.mult
                )
        nc.scalar.activation(out=warm[:, 1:2], in_=silu[:, 0:1], func=ACT.Abs_reciprocal_sqrt, bias=1.0)

        w2_rounded = keep.tile([P, N, PACK], BF16, name="w2_rounded", align_bytes=64)
        w2_codes = keep.tile([P, N], U32, name="w2_codes", align_bytes=64)
        w2_plane = keep.tile([P, N], U8, name="w2_plane", align_bytes=64)
        nc.scalar.copy(
            out=w2_rounded[:].rearrange("p (c e) i -> p c i e", e=2),
            in_=w2_raw[:].rearrange("p i (c e) -> p c i e", e=2),
        )
        for first, last in ((0, BANK), (BANK, N)):
            nc.vector.quantize_mx(
                out=w2_codes[:, first:last].bitcast(E4M3),
                scales=w2_plane[:, first:last],
                in_=w2_rounded[:, first:last, :].rearrange("p n i -> p (n i)"),
            )

        z_codes = keep.tile([P, M], U32, name="z_codes", align_bytes=64)
        z_plane = keep.tile([P, M], U8, name="z_plane", align_bytes=64)
        result = [keep.tile([P, N_TILES, BANK], F32, name="result%d" % half) for half in range(M // BANK)]
        x = {}
        z = {}

        def result_part(lo, hi, first, width):
            return result[first // BANK][:, lo:hi, first % BANK : first % BANK + width]

        def read_page(c, t):
            if t == 0:
                x[c] = pairs.tile([P, PACK, CHUNK], F32, name="x")
            nc.vector.tensor_tensor(
                x[c][:, t, :],
                pages[t][:].indirect(entries(session, c * CHUNK, CHUNK)),
                wgt_sb[:, c * CHUNK : (c + 1) * CHUNK],
                ALU.mult,
            )

        def subtract(c):
            z[c] = pairs.tile([P, CHUNK, PACK], BF16, name="z", align_bytes=64)
            nc.vector.tensor_tensor(
                z[c][:].rearrange("p (c e) t -> p c t e", e=2),
                x[c][:].rearrange("p t (c e) -> p c t e", e=2),
                press_sb[:, :, c * CHUNK : (c + 1) * CHUNK].rearrange("p t (c e) -> p c t e", e=2),
                ALU.subtract,
            )

        def quantise_z(c):
            cols = slice(c * CHUNK, (c + 1) * CHUNK)
            nc.vector.quantize_mx(
                out=z_codes[:, cols].bitcast(E4M3), scales=z_plane[:, cols], in_=z[c][:].rearrange("p m t -> p (m t)")
            )

        root_chunk = CHUNKS - 2

        def damping(c):
            cols = slice(c * CHUNK, (c + 1) * CHUNK)
            for lo, hi in TILE_GROUPS:
                strain = strain_banks.tile([P, hi - lo, CHUNK], F32, name="bank")
                for n in range(lo, hi):
                    nc.tensor.matmul_mx(
                        out=strain[:, n - lo, :],
                        lhsT=w4_codes[:, 2 * n * P : 2 * (n + 1) * P].bitcast(E2M1),
                        lhsT_scale=w4_plane[:, n * P : (n + 1) * P],
                        rhs=z_codes[:, cols].bitcast(E4M3),
                        rhs_scale=z_plane[:, cols],
                        start=True,
                        stop=True,
                    )
                nc.scalar.activation(out=result_part(lo, hi, c * CHUNK, CHUNK), in_=strain[:], func=ACT.Abs)
            spans = TILE_GROUPS if c == CHUNKS - 1 else [(0, N_TILES - 1), (N_TILES - 1, N_TILES)]
            parts = [result_part(lo, hi, c * CHUNK, CHUNK) for lo, hi in spans]
            for part in parts:
                nc.scalar.activation(out=part, in_=part, func=ACT.Abs_reciprocal_sqrt, bias=1.0)
            if c != root_chunk:
                for part in parts:
                    nc.scalar.activation(out=part, in_=part, func=ACT.Square)

        def response(lo, hi, first, width):
            cols = slice(first, first + width)
            resp = resp_banks.tile([P, hi - lo, width], F32, name="bank")
            for n in range(lo, hi):
                nc.tensor.matmul_mx(
                    out=resp[:, n - lo, :],
                    lhsT=w2_codes[:, n * P : (n + 1) * P].bitcast(E4M3),
                    lhsT_scale=w2_plane[:, n * P : (n + 1) * P],
                    rhs=z_codes[:, cols].bitcast(E4M3),
                    rhs_scale=z_plane[:, cols],
                    start=True,
                    stop=True,
                )
            return resp

        def damp_and_store(values, lo, hi, first, width):
            part = result_part(lo, hi, first, width)
            nc.vector.tensor_tensor(part, values[:], part, ALU.mult)
            rows = out[lo * P : hi * P, first : first + width]
            nc.sync.dma_start(out=rows.rearrange("(n p) m -> p n m", p=P), in_=part)

        for t in range(PACK):
            read_page(0, t)
        for c in range(CHUNKS):
            more = c + 1 < CHUNKS
            if more:
                read_page(c + 1, 0)
            subtract(c)
            if more:
                read_page(c + 1, 1)
            quantise_z(c)
            damping(c)
            if more:
                read_page(c + 1, 2)
                read_page(c + 1, 3)

        for n in range(N_TILES):
            damp_and_store(response(n, n + 1, 0, BANK), n, n + 1, 0, BANK)
        first = root_chunk * CHUNK
        halfway = []
        for lo, hi in TILE_GROUPS:
            resp = response(lo, hi, first, CHUNK)
            once = triples.tile([P, hi - lo, CHUNK], F32, name="once")
            nc.vector.tensor_tensor(once[:], resp[:], result_part(lo, hi, first, CHUNK), ALU.mult)
            halfway.append(once)
        for (lo, hi), once in zip(TILE_GROUPS, halfway):
            damp_and_store(once, lo, hi, first, CHUNK)
        first = (CHUNKS - 1) * CHUNK
        for lo, hi in TILE_GROUPS:
            damp_and_store(response(lo, hi, first, CHUNK), lo, hi, first, CHUNK)
